import numpy as np
import ml_dtypes


def mxq(x, axis, fmt="e4m3"):
    dtype, down = {"e4m3": (ml_dtypes.float8_e4m3fn, 7), "e5m2": (ml_dtypes.float8_e5m2, 14)}[fmt]
    v = np.moveaxis(np.asarray(x, np.float32).astype(ml_dtypes.bfloat16).astype(np.float64), axis, -1)
    blocks = v.reshape(v.shape[:-1] + (-1, 32))
    amax = np.abs(blocks).max(-1, keepdims=True)
    byte = np.maximum(np.where(amax > 0, np.frexp(amax)[1] - 1 + 127, 0) - down, 1)
    scale = np.exp2(byte - 127.0)
    codes = (blocks / scale).astype(np.float32).astype(dtype).astype(np.float64)
    return np.moveaxis((codes * scale).reshape(v.shape), -1, axis)


WIDE = False


def mx_kscale(k):
    if not WIDE:
        return np.ones(k)
    levels = np.array([30, -30])
    if k % 512:
        return np.exp2(np.random.permutation(np.resize(levels, k // 32))).repeat(32)
    a = np.empty((k // 512, 16))
    for p in range(k // 512):
        a[p, :8] = np.random.permutation(np.resize(levels, 8))
        for g in range(8):
            far = levels[np.abs(levels - a[p, g]) >= 10]
            a[p, g + 8] = far[np.random.randint(len(far))]
    return np.exp2(a.ravel()).repeat(32)


def f64(x):
    return np.asarray(x).astype(np.float64)


def striped(idx):
    return np.tile(np.asarray(idx).reshape(-1, 16).T, (8, 1)).astype(np.uint16)


def unstriped(offs):
    return offs[:16].T.reshape(-1).astype(np.int64)


E2M1 = np.array([0.0, 0.5, 1.0, 1.5, 2.0, 3.0, 4.0, 6.0, -0.0, -0.5, -1.0, -1.5, -2.0, -3.0, -4.0, -6.0])


def pack_weight(w, fmt):
    k, n = w.shape
    w = f64(np.asarray(w, np.float32).astype(ml_dtypes.bfloat16)).reshape(k // 32, 32, n)
    amax = np.abs(w).max(1)
    if fmt in ("e4m3", "e5m2"):
        byte = np.frexp(amax)[1] - 1 + 127 - (7 if fmt == "e4m3" else 14)
    else:
        mant, ex = np.frexp(amax / 6.0)
        byte = np.where(mant > 0.5, ex, ex - 1) + 127
    byte = np.clip(np.where(amax > 0, byte, 1), 1, 254)
    scaled = (w * np.exp2(127.0 - byte)[:, None, :]).reshape(k, n).astype(np.float32)
    by_word = np.ascontiguousarray(scaled.reshape(k // 512, 128, 4, n).transpose(0, 1, 3, 2))
    if fmt in ("e4m3", "e5m2"):
        words = by_word.astype(ml_dtypes.float8_e4m3fn if fmt == "e4m3" else ml_dtypes.float8_e5m2).view(np.uint8)
    else:
        c = by_word.astype(ml_dtypes.float4_e2m1fn).view(np.uint8) & 0xF
        words = (c[..., 0::2] | (c[..., 1::2] << 4)).reshape(k // 512, 128, 2 * n)
    return np.ascontiguousarray(words), np.ascontiguousarray(byte.astype(np.uint8).reshape(k // 512, 16, n))


def unpack_weight(words, scales, fmt):
    g, _, n = scales.shape
    words = np.ascontiguousarray(words).reshape(g, 128, n, -1)
    if fmt in ("e4m3", "e5m2"):
        vals = words.view(ml_dtypes.float8_e4m3fn if fmt == "e4m3" else ml_dtypes.float8_e5m2).astype(np.float64)
    else:
        nib = np.empty((g, 128, n, 4), np.uint8)
        nib[..., 0::2] = words & 0xF
        nib[..., 1::2] = words >> 4
        vals = E2M1[nib]
    vals = vals * np.repeat(np.exp2(scales.astype(np.float64) - 127.0), 8, axis=1)[..., None]
    return vals.transpose(0, 1, 3, 2).reshape(g * 512, n)


def e4m3fn_bytes(y):
    return np.clip(np.asarray(y, np.float64), -448.0, 448.0).astype(np.float32).astype(ml_dtypes.float8_e4m3fn).view(np.uint8)


def e4m3fn_values(b):
    return np.asarray(b, np.uint8).view(ml_dtypes.float8_e4m3fn).astype(np.float64)


K, V, O, U, F, T, Z = 512, 1024, 256, 256, 512, 1024, 1024


def setup_inputs():
    n = np.random.standard_normal
    idx = np.random.permutation(V)[:O]
    idx2 = np.random.permutation(V)[:U]
    idx3 = np.random.permutation(T)[:O]
    idx4 = np.random.permutation(Z)[:U]
    fk = mx_kscale(K)
    ff = mx_kscale(F)
    xtp = pack_weight(n((F, T)) / ff[:, None], "e5m2")
    xop = pack_weight(n((F, Z)) * 1 / np.sqrt(F) * ff[:, None], "e4m3")
    return {
        "ca": e4m3fn_bytes(60.0 * n((K, V))),
        "sa": (np.random.uniform(0.004, 0.012, (K, 1)) * fk[:, None]).astype(np.float32),
        "sb": (np.random.uniform(0.0002, 0.0006, (K, 1)) / fk[:, None]).astype(np.float32),
        "xt_words": xtp[0],
        "xt_scales": xtp[1],
        "xo_words": xop[0],
        "xo_scales": xop[1],
        "offs": striped(idx),
        "offs2": striped(idx2),
        "offs3": striped(idx3),
        "offs4": striped(idx4),
    }


def reference(ca, sa, sb, xt_words, xt_scales, xo_words, xo_scales, offs, offs2, offs3, offs4):
    idx = unstriped(offs)
    idx2 = unstriped(offs2)
    idx3 = unstriped(offs3)
    idx4 = unstriped(offs4)
    xtu = unpack_weight(xt_words, xt_scales, "e5m2")
    xou = unpack_weight(xo_words, xo_scales, "e4m3")
    z1 = e4m3fn_values(ca)[:, idx] * f64(sa)
    z2 = e4m3fn_values(ca)[:, idx2] * f64(sb)
    z1q = mxq(z1, 0, "e4m3")
    z2q = mxq(z2, 0, "e4m3")
    xtidx3g = xtu[:, idx3]
    xoidx4g = xou[:, idx4]
    p = z1q.T @ z2q + xtidx3g.T @ xoidx4g
    return p

@@ -1,0 +1,108 @@
+from contextlib import ExitStack
+
+import concourse.mybir as mybir
+
+K, V, O, U, F = 512, 1024, 256, 256, 512
+FLOPS = 2 * K * O * U + 2 * F * O * U
+
+F32 = mybir.dt.float32
+BF16 = mybir.dt.bfloat16
+I32 = mybir.dt.int32
+U32 = mybir.dt.uint32
+U16 = mybir.dt.uint16
+U8 = mybir.dt.uint8
+FP8 = mybir.dt.float8_e4m3fn
+E4M3X4 = mybir.dt.float8_e4m3fn_x4
+E5M2X4 = mybir.dt.float8_e5m2_x4
+COPY = mybir.ActivationFunctionType.Copy
+
+P = 128
+PACK = 4
+N = 256
+
+
+def tile_list_hybridscores_kernel(tc, ca, sa, sb, xt_words, xt_scales, xo_words, xo_scales, offs, offs2, offs3, offs4, out):
+    nc = tc.nc
+    with ExitStack() as ctx:
+        sb_pool = ctx.enter_context(tc.tile_pool(name="sbuf", bufs=1))
+        psum = ctx.enter_context(tc.psum_pool(name="psum", bufs=1))
+
+        def tile(name, shape, dtype):
+            return sb_pool.tile(shape, dtype, name=name, align_bytes=64)
+
+        def load_list(name, src):
+            t = tile(name, [P, N // 16], U16)
+            nc.sync.dma_start(t[:], src)
+            return t
+
+        xt_srows = tile("xt_srows", [P, V], U8)
+        xo_srows = tile("xo_srows", [P, V], U8)
+        nc.vector.memset(xo_srows[:].bitcast(U32), 0)
+        nc.vector.memset(xt_srows[:].bitcast(U32), 0)
+
+        list1 = load_list("list1", offs)
+        ca_rows = ca.rearrange("(p t) v -> p t v", t=PACK)
+        table = []
+        for t in range(PACK):
+            tt = tile("table%d" % t, [P, V], U8)
+            nc.sync.dma_start(tt[:], ca_rows[:, t, :])
+            table.append(tt)
+        sa_t = tile("sa_t", [P, PACK], F32)
+        nc.scalar.dma_start(sa_t[:], sa.rearrange("(p t) o -> p (t o)", t=PACK))
+        list2 = load_list("list2", offs2)
+        sb_t = tile("sb_t", [P, PACK], F32)
+        nc.scalar.dma_start(sb_t[:], sb.rearrange("(p t) o -> p (t o)", t=PACK))
+
+        xo_w = tile("xo_w", [P, V], U32)
+        xt_w = tile("xt_w", [P, V], U32)
+        list4 = load_list("list4", offs4)
+        nc.sync.dma_start(xo_w[:].bitcast(I32), xo_words[0].rearrange("p n t -> p (n t)").bitcast(I32))
+        list3 = load_list("list3", offs3)
+        nc.sync.dma_start(xt_w[:].bitcast(I32), xt_words[0].rearrange("p n t -> p (n t)").bitcast(I32))
+        for rows, src in ((xo_srows, xo_scales), (xt_srows, xt_scales)):
+            for q in range(4):
+                nc.sync.dma_start(rows[32 * q : 32 * q + 4, :].bitcast(I32), src[0, 4 * q : 4 * q + 4, :].bitcast(I32))
+
+        def gather(name, window, offsets, dtype):
+            g = tile(name, [P, N], dtype)
+            nc.vector.tensor_copy(g[:], window[:].indirect(offsets[:]))
+            return g
+
+        def scaled(name, offsets, step):
+            planes = tile(name + "_planes", [P, PACK, N], BF16)
+            for t in range(PACK):
+                g = gather("%s_bytes%d" % (name, t), table[t], offsets, U8)
+                nc.scalar.activation(out=planes[:, t, :], in_=g[:].bitcast(FP8), func=COPY, scale=step[:, t : t + 1])
+            woven = tile(name + "_woven", [P, N, PACK], BF16)
+            nc.scalar.copy(out=woven[:], in_=planes[:].rearrange("p t c -> p c t"))
+            return woven
+
+        def quantize(name, woven):
+            codes = tile(name + "_codes", [P, N], U32)
+            scales = tile(name + "_scales", [P, N], U8)
+            nc.vector.quantize_mx(out=codes[:].bitcast(E4M3X4), scales=scales[:], in_=woven[:].rearrange("p c t -> p (c t)"))
+            return codes, scales
+
+        z1 = scaled("z1", list1, sa_t)
+        z2 = scaled("z2", list2, sb_t)
+        z1_codes, z1_scales = quantize("z1", z1)
+        xo_g = gather("xo_g", xo_w, list4, U32)
+        xt_g = gather("xt_g", xt_w, list3, U32)
+        xo_s = gather("xo_s", xo_srows, list4, U8)
+        z2_codes, z2_scales = quantize("z2", z2)
+        xt_s = gather("xt_s", xt_srows, list3, U8)
+
+        for h in range(O // P):
+            cols = slice(h * P, (h + 1) * P)
+            acc = psum.tile([P, U], F32, name="acc%d" % h)
+            nc.tensor.matmul_mx(out=acc[:], lhsT=z1_codes[:, cols].bitcast(E4M3X4), lhsT_scale=z1_scales[:, cols],
+                                rhs=z2_codes[:].bitcast(E4M3X4), rhs_scale=z2_scales[:], start=True, stop=False)
+            nc.tensor.matmul_mx(out=acc[:], lhsT=xt_g[:, cols].bitcast(E5M2X4), lhsT_scale=xt_s[:, cols],
+                                rhs=xo_g[:].bitcast(E4M3X4), rhs_scale=xo_s[:], start=False, stop=True)
+            res = tile("res%d" % h, [P, U], F32)
+            if h == 0:
+                nc.vector.tensor_copy(res[:], acc[:])
+                nc.sync.dma_start(out[cols, :], res[:])
+            else:
+                nc.scalar.copy(res[:], acc[:])
+                nc.scalar.dma_start(out[cols, :], res[:])

@@ -27,82 +27,105 @@ def tile_list_hybridscores_kernel(tc, ca, sa, sb, xt_words, xt_scales, xo_words,
         sb_pool = ctx.enter_context(tc.tile_pool(name="sbuf", bufs=1))
         psum = ctx.enter_context(tc.psum_pool(name="psum", bufs=1))
 
-        def tile(name, shape, dtype):
-            return sb_pool.tile(shape, dtype, name=name, align_bytes=64)
+        def tile(name, shape, dtype, tag=None):
+            return sb_pool.tile(shape, dtype, name=name, tag=tag or name, align_bytes=64)
 
         def load_list(name, src):
             t = tile(name, [P, N // 16], U16)
             nc.sync.dma_start(t[:], src)
             return t
 
+        def load_scale_rows(queue, rows, src):
+            for q in range(4):
+                queue.dma_start(rows[32 * q : 32 * q + 4, :].bitcast(I32), src[0, 4 * q : 4 * q + 4, :].bitcast(I32))
+
         xt_srows = tile("xt_srows", [P, V], U8)
         xo_srows = tile("xo_srows", [P, V], U8)
-        nc.vector.memset(xo_srows[:].bitcast(U32), 0)
         nc.vector.memset(xt_srows[:].bitcast(U32), 0)
+        nc.vector.memset(xo_srows[:].bitcast(U32), 0)
 
-        list1 = load_list("list1", offs)
         ca_rows = ca.rearrange("(p t) v -> p t v", t=PACK)
         table = []
         for t in range(PACK):
             tt = tile("table%d" % t, [P, V], U8)
             nc.sync.dma_start(tt[:], ca_rows[:, t, :])
             table.append(tt)
-        sa_t = tile("sa_t", [P, PACK], F32)
-        nc.scalar.dma_start(sa_t[:], sa.rearrange("(p t) o -> p (t o)", t=PACK))
-        list2 = load_list("list2", offs2)
+            if t == 0:
+                list2 = load_list("list2", offs2)
         sb_t = tile("sb_t", [P, PACK], F32)
         nc.scalar.dma_start(sb_t[:], sb.rearrange("(p t) o -> p (t o)", t=PACK))
+        list1 = load_list("list1", offs)
+        sa_t = tile("sa_t", [P, PACK], F32)
+        nc.scalar.dma_start(sa_t[:], sa.rearrange("(p t) o -> p (t o)", t=PACK))
 
         xo_w = tile("xo_w", [P, V], U32)
         xt_w = tile("xt_w", [P, V], U32)
-        list4 = load_list("list4", offs4)
         nc.sync.dma_start(xo_w[:].bitcast(I32), xo_words[0].rearrange("p n t -> p (n t)").bitcast(I32))
         list3 = load_list("list3", offs3)
         nc.sync.dma_start(xt_w[:].bitcast(I32), xt_words[0].rearrange("p n t -> p (n t)").bitcast(I32))
-        for rows, src in ((xo_srows, xo_scales), (xt_srows, xt_scales)):
-            for q in range(4):
-                nc.sync.dma_start(rows[32 * q : 32 * q + 4, :].bitcast(I32), src[0, 4 * q : 4 * q + 4, :].bitcast(I32))
+        load_scale_rows(nc.sync, xo_srows, xo_scales)
+        list4 = load_list("list4", offs4)
+        load_scale_rows(nc.sync, xt_srows, xt_scales)
 
-        def gather(name, window, offsets, dtype):
-            g = tile(name, [P, N], dtype)
-            nc.vector.tensor_copy(g[:], window[:].indirect(offsets[:]))
+        def gather(name, window, offsets, dtype, tag=None):
+            g = tile(name, [P, 16 * offsets.shape[1]], dtype, tag)
+            nc.vector.tensor_copy(g[:], window[:].indirect(offsets))
             return g
 
         def scaled(name, offsets, step):
-            planes = tile(name + "_planes", [P, PACK, N], BF16)
+            planes = tile(name + "_planes", [P, PACK, N], BF16, "planes")
             for t in range(PACK):
-                g = gather("%s_bytes%d" % (name, t), table[t], offsets, U8)
+                g = gather("%s_bytes%d" % (name, t), table[t], offsets[:], U8)
                 nc.scalar.activation(out=planes[:, t, :], in_=g[:].bitcast(FP8), func=COPY, scale=step[:, t : t + 1])
-            woven = tile(name + "_woven", [P, N, PACK], BF16)
-            nc.scalar.copy(out=woven[:], in_=planes[:].rearrange("p t c -> p c t"))
+            return planes
+
+        def weave(name, planes):
+            woven = tile(name + "_woven", [P, planes.shape[2], PACK], BF16)
+            nc.scalar.copy(out=woven[:].rearrange("p (c i) t -> p c t i", i=4), in_=planes.rearrange("p t (c i) -> p c t i", i=4))
             return woven
 
-        def quantize(name, woven):
-            codes = tile(name + "_codes", [P, N], U32)
-            scales = tile(name + "_scales", [P, N], U8)
-            nc.vector.quantize_mx(out=codes[:].bitcast(E4M3X4), scales=scales[:], in_=woven[:].rearrange("p c t -> p (c t)"))
-            return codes, scales
+        def quantize(codes, scales, woven):
+            nc.vector.quantize_mx(out=codes.bitcast(E4M3X4), scales=scales, in_=woven[:].rearrange("p c t -> p (c t)"))
 
-        z1 = scaled("z1", list1, sa_t)
-        z2 = scaled("z2", list2, sb_t)
-        z1_codes, z1_scales = quantize("z1", z1)
-        xo_g = gather("xo_g", xo_w, list4, U32)
-        xt_g = gather("xt_g", xt_w, list3, U32)
-        xo_s = gather("xo_s", xo_srows, list4, U8)
-        z2_codes, z2_scales = quantize("z2", z2)
-        xt_s = gather("xt_s", xt_srows, list3, U8)
+        z2 = weave("z2", scaled("z2", list2, sb_t)[:])
+        z1_planes = scaled("z1", list1, sa_t)
+        z1 = [weave("z1_%d" % h, z1_planes[:, :, h * P : (h + 1) * P]) for h in range(2)]
 
-        for h in range(O // P):
-            cols = slice(h * P, (h + 1) * P)
-            acc = psum.tile([P, U], F32, name="acc%d" % h)
-            nc.tensor.matmul_mx(out=acc[:], lhsT=z1_codes[:, cols].bitcast(E4M3X4), lhsT_scale=z1_scales[:, cols],
-                                rhs=z2_codes[:].bitcast(E4M3X4), rhs_scale=z2_scales[:], start=True, stop=False)
-            nc.tensor.matmul_mx(out=acc[:], lhsT=xt_g[:, cols].bitcast(E5M2X4), lhsT_scale=xt_s[:, cols],
-                                rhs=xo_g[:].bitcast(E4M3X4), rhs_scale=xo_s[:], start=False, stop=True)
-            res = tile("res%d" % h, [P, U], F32)
-            if h == 0:
-                nc.vector.tensor_copy(res[:], acc[:])
-                nc.sync.dma_start(out[cols, :], res[:])
-            else:
-                nc.scalar.copy(res[:], acc[:])
-                nc.scalar.dma_start(out[cols, :], res[:])
+        z2_codes = tile("z2_codes", [P, N], U32)
+        z2_scales = tile("z2_scales", [P, N], U8)
+        quantize(z2_codes[:], z2_scales[:], z2)
+        xt_g = gather("xt_g", xt_w, list3[:], U32)
+        xo_g = gather("xo_g", xo_w, list4[:], U32)
+        xo_s = gather("xo_s", xo_srows, list4[:], U8)
+        z1_codes = tile("z1_codes", [P, N], U32, "xo_w")
+        z1_scales = tile("z1_scales", [P, N], U8)
+        for h in range(2):
+            quantize(z1_codes[:, h * P : (h + 1) * P], z1_scales[:, h * P : (h + 1) * P], z1[h])
+        xt_s = [gather("xt_s%d" % h, xt_srows, list3[:, 8 * h : 8 * h + 8], U8) for h in range(2)]
+
+        def codes_pass(acc, h, ucols, start):
+            nc.tensor.matmul_mx(out=acc[:], lhsT=z1_codes[:, h * P : (h + 1) * P].bitcast(E4M3X4), lhsT_scale=z1_scales[:, h * P : (h + 1) * P],
+                                rhs=z2_codes[:, ucols].bitcast(E4M3X4), rhs_scale=z2_scales[:, ucols], start=start, stop=not start)
+
+        def vectors_pass(acc, h, ucols, start):
+            nc.tensor.matmul_mx(out=acc[:], lhsT=xt_g[:, h * P : (h + 1) * P].bitcast(E5M2X4), lhsT_scale=xt_s[h][:],
+                                rhs=xo_g[:, ucols].bitcast(E4M3X4), rhs_scale=xo_s[:, ucols], start=start, stop=not start)
+
+        acc0 = psum.tile([P, U], F32, name="acc0")
+        acc1 = psum.tile([P, P], F32, name="acc1")
+        acc2 = psum.tile([P, P], F32, name="acc2")
+        codes_pass(acc0, 0, slice(0, U), True)
+        codes_pass(acc1, 1, slice(0, P), True)
+        codes_pass(acc2, 1, slice(P, U), True)
+        vectors_pass(acc0, 0, slice(0, U), False)
+        vectors_pass(acc1, 1, slice(0, P), False)
+        vectors_pass(acc2, 1, slice(P, U), False)
+        res0 = tile("res0", [P, U], F32)
+        res1 = tile("res1", [P, P], F32)
+        res2 = tile("res2", [P, P], F32)
+        nc.scalar.copy(res0[:], acc0[:])
+        nc.sync.dma_start(out[0:P, :], res0[:])
+        nc.scalar.copy(res1[:], acc1[:])
+        nc.scalar.dma_start(out[P:O, 0:P], res1[:])
+        nc.vector.tensor_copy(res2[:], acc2[:])
+        nc.sync.dma_start(out[P:O, P:U], res2[:])

@@ -60,12 +60,12 @@ def tile_list_hybridscores_kernel(tc, ca, sa, sb, xt_words, xt_scales, xo_words,
 
         xo_w = tile("xo_w", [P, V], U32)
         xt_w = tile("xt_w", [P, V], U32)
-        nc.sync.dma_start(xo_w[:].bitcast(I32), xo_words[0].rearrange("p n t -> p (n t)").bitcast(I32))
         list3 = load_list("list3", offs3)
+        load_scale_rows(nc.sync, xt_srows, xt_scales)
         nc.sync.dma_start(xt_w[:].bitcast(I32), xt_words[0].rearrange("p n t -> p (n t)").bitcast(I32))
+        nc.sync.dma_start(xo_w[:].bitcast(I32), xo_words[0].rearrange("p n t -> p (n t)").bitcast(I32))
         load_scale_rows(nc.sync, xo_srows, xo_scales)
         list4 = load_list("list4", offs4)
-        load_scale_rows(nc.sync, xt_srows, xt_scales)
 
         def gather(name, window, offsets, dtype, tag=None):
             g = tile(name, [P, 16 * offsets.shape[1]], dtype, tag)
@@ -94,30 +94,32 @@ def tile_list_hybridscores_kernel(tc, ca, sa, sb, xt_words, xt_scales, xo_words,
         z2_codes = tile("z2_codes", [P, N], U32)
         z2_scales = tile("z2_scales", [P, N], U8)
         quantize(z2_codes[:], z2_scales[:], z2)
-        xt_g = gather("xt_g", xt_w, list3[:], U32)
+        xt_g = [gather("xt_g0", xt_w, list3[:, 0:8], U32)]
+        xt_s = [gather("xt_s0", xt_srows, list3[:, 0:8], U8)]
         xo_g = gather("xo_g", xo_w, list4[:], U32)
         xo_s = gather("xo_s", xo_srows, list4[:], U8)
         z1_codes = tile("z1_codes", [P, N], U32, "xo_w")
         z1_scales = tile("z1_scales", [P, N], U8)
         for h in range(2):
             quantize(z1_codes[:, h * P : (h + 1) * P], z1_scales[:, h * P : (h + 1) * P], z1[h])
-        xt_s = [gather("xt_s%d" % h, xt_srows, list3[:, 8 * h : 8 * h + 8], U8) for h in range(2)]
+        xt_g.append(gather("xt_g1", xt_w, list3[:, 8:16], U32, "z1_0_woven"))
+        xt_s.append(gather("xt_s1", xt_srows, list3[:, 8:16], U8, "z1_1_woven"))
 
         def codes_pass(acc, h, ucols, start):
             nc.tensor.matmul_mx(out=acc[:], lhsT=z1_codes[:, h * P : (h + 1) * P].bitcast(E4M3X4), lhsT_scale=z1_scales[:, h * P : (h + 1) * P],
                                 rhs=z2_codes[:, ucols].bitcast(E4M3X4), rhs_scale=z2_scales[:, ucols], start=start, stop=not start)
 
         def vectors_pass(acc, h, ucols, start):
-            nc.tensor.matmul_mx(out=acc[:], lhsT=xt_g[:, h * P : (h + 1) * P].bitcast(E5M2X4), lhsT_scale=xt_s[h][:],
+            nc.tensor.matmul_mx(out=acc[:], lhsT=xt_g[h][:].bitcast(E5M2X4), lhsT_scale=xt_s[h][:],
                                 rhs=xo_g[:, ucols].bitcast(E4M3X4), rhs_scale=xo_s[:, ucols], start=start, stop=not start)
 
         acc0 = psum.tile([P, U], F32, name="acc0")
         acc1 = psum.tile([P, P], F32, name="acc1")
         acc2 = psum.tile([P, P], F32, name="acc2")
-        codes_pass(acc0, 0, slice(0, U), True)
+        vectors_pass(acc0, 0, slice(0, U), True)
+        codes_pass(acc0, 0, slice(0, U), False)
         codes_pass(acc1, 1, slice(0, P), True)
         codes_pass(acc2, 1, slice(P, U), True)
-        vectors_pass(acc0, 0, slice(0, U), False)
         vectors_pass(acc1, 1, slice(0, P), False)
         vectors_pass(acc2, 1, slice(P, U), False)
         res0 = tile("res0", [P, U], F32)

@@ -52,11 +52,11 @@ def tile_list_hybridscores_kernel(tc, ca, sa, sb, xt_words, xt_scales, xo_words,
             table.append(tt)
             if t == 0:
                 list2 = load_list("list2", offs2)
-        sb_t = tile("sb_t", [P, PACK], F32)
-        nc.scalar.dma_start(sb_t[:], sb.rearrange("(p t) o -> p (t o)", t=PACK))
+                sb_t = tile("sb_t", [P, PACK], F32)
+                nc.sync.dma_start(sb_t[:], sb.rearrange("(p t) o -> p (t o)", t=PACK))
         list1 = load_list("list1", offs)
         sa_t = tile("sa_t", [P, PACK], F32)
-        nc.scalar.dma_start(sa_t[:], sa.rearrange("(p t) o -> p (t o)", t=PACK))
+        nc.sync.dma_start(sa_t[:], sa.rearrange("(p t) o -> p (t o)", t=PACK))
 
         xo_w = tile("xo_w", [P, V], U32)
         xt_w = tile("xt_w", [P, V], U32)

@@ -73,7 +73,7 @@ def tile_list_hybridscores_kernel(tc, ca, sa, sb, xt_words, xt_scales, xo_words,
             return g
 
         def scaled(name, offsets, step):
-            planes = tile(name + "_planes", [P, PACK, N], BF16, "planes")
+            planes = tile(name + "_planes", [P, PACK, N], BF16)
             for t in range(PACK):
                 g = gather("%s_bytes%d" % (name, t), table[t], offsets[:], U8)
                 nc.scalar.activation(out=planes[:, t, :], in_=g[:].bitcast(FP8), func=COPY, scale=step[:, t : t + 1])
@@ -102,8 +102,8 @@ def tile_list_hybridscores_kernel(tc, ca, sa, sb, xt_words, xt_scales, xo_words,
         z1_scales = tile("z1_scales", [P, N], U8)
         for h in range(2):
             quantize(z1_codes[:, h * P : (h + 1) * P], z1_scales[:, h * P : (h + 1) * P], z1[h])
-        xt_g.append(gather("xt_g1", xt_w, list3[:, 8:16], U32, "z1_0_woven"))
-        xt_s.append(gather("xt_s1", xt_srows, list3[:, 8:16], U8, "z1_1_woven"))
+        xt_g.append(gather("xt_g1", xt_w, list3[:, 8:16], U32, "xo_srows"))
+        xt_s.append(gather("xt_s1", xt_srows, list3[:, 8:16], U8, "z1_0_woven"))
 
         def codes_pass(acc, h, ucols, start):
             nc.tensor.matmul_mx(out=acc[:], lhsT=z1_codes[:, h * P : (h + 1) * P].bitcast(E4M3X4), lhsT_scale=z1_scales[:, h * P : (h + 1) * P],

from contextlib import ExitStack

import concourse.mybir as mybir

K, V, O, U, F = 512, 1024, 256, 256, 512
FLOPS = 2 * K * O * U + 2 * F * O * U

F32 = mybir.dt.float32
BF16 = mybir.dt.bfloat16
I32 = mybir.dt.int32
U32 = mybir.dt.uint32
U16 = mybir.dt.uint16
U8 = mybir.dt.uint8
FP8 = mybir.dt.float8_e4m3fn
E4M3X4 = mybir.dt.float8_e4m3fn_x4
E5M2X4 = mybir.dt.float8_e5m2_x4
COPY = mybir.ActivationFunctionType.Copy

P = 128
PACK = 4
N = 256


def tile_list_hybridscores_kernel(tc, ca, sa, sb, xt_words, xt_scales, xo_words, xo_scales, offs, offs2, offs3, offs4, out):
    nc = tc.nc
    with ExitStack() as ctx:
        sb_pool = ctx.enter_context(tc.tile_pool(name="sbuf", bufs=1))
        psum = ctx.enter_context(tc.psum_pool(name="psum", bufs=1))

        def tile(name, shape, dtype, tag=None):
            return sb_pool.tile(shape, dtype, name=name, tag=tag or name, align_bytes=64)

        def load_list(name, src):
            t = tile(name, [P, N // 16], U16)
            nc.sync.dma_start(t[:], src)
            return t

        def load_scale_rows(queue, rows, src):
            for q in range(4):
                queue.dma_start(rows[32 * q : 32 * q + 4, :].bitcast(I32), src[0, 4 * q : 4 * q + 4, :].bitcast(I32))

        xt_srows = tile("xt_srows", [P, V], U8)
        xo_srows = tile("xo_srows", [P, V], U8)
        nc.vector.memset(xt_srows[:].bitcast(U32), 0)
        nc.vector.memset(xo_srows[:].bitcast(U32), 0)

        ca_rows = ca.rearrange("(p t) v -> p t v", t=PACK)
        table = []
        for t in range(PACK):
            tt = tile("table%d" % t, [P, V], U8)
            nc.sync.dma_start(tt[:], ca_rows[:, t, :])
            table.append(tt)
            if t == 0:
                list2 = load_list("list2", offs2)
                sb_t = tile("sb_t", [P, PACK], F32)
                nc.sync.dma_start(sb_t[:], sb.rearrange("(p t) o -> p (t o)", t=PACK))
        list1 = load_list("list1", offs)
        sa_t = tile("sa_t", [P, PACK], F32)
        nc.sync.dma_start(sa_t[:], sa.rearrange("(p t) o -> p (t o)", t=PACK))

        xo_w = tile("xo_w", [P, V], U32)
        xt_w = tile("xt_w", [P, V], U32)
        list3 = load_list("list3", offs3)
        load_scale_rows(nc.sync, xt_srows, xt_scales)
        nc.sync.dma_start(xt_w[:].bitcast(I32), xt_words[0].rearrange("p n t -> p (n t)").bitcast(I32))
        nc.sync.dma_start(xo_w[:].bitcast(I32), xo_words[0].rearrange("p n t -> p (n t)").bitcast(I32))
        load_scale_rows(nc.sync, xo_srows, xo_scales)
        list4 = load_list("list4", offs4)

        def gather(name, window, offsets, dtype, tag=None):
            g = tile(name, [P, 16 * offsets.shape[1]], dtype, tag)
            nc.vector.tensor_copy(g[:], window[:].indirect(offsets))
            return g

        def scaled(name, offsets, step):
            planes = tile(name + "_planes", [P, PACK, N], BF16)
            for t in range(PACK):
                g = gather("%s_bytes%d" % (name, t), table[t], offsets[:], U8)
                nc.scalar.activation(out=planes[:, t, :], in_=g[:].bitcast(FP8), func=COPY, scale=step[:, t : t + 1])
            return planes

        def weave(name, planes):
            woven = tile(name + "_woven", [P, planes.shape[2], PACK], BF16)
            nc.scalar.copy(out=woven[:].rearrange("p (c i) t -> p c t i", i=4), in_=planes.rearrange("p t (c i) -> p c t i", i=4))
            return woven

        def quantize(codes, scales, woven):
            nc.vector.quantize_mx(out=codes.bitcast(E4M3X4), scales=scales, in_=woven[:].rearrange("p c t -> p (c t)"))

        z2 = weave("z2", scaled("z2", list2, sb_t)[:])
        z1_planes = scaled("z1", list1, sa_t)
        z1 = [weave("z1_%d" % h, z1_planes[:, :, h * P : (h + 1) * P]) for h in range(2)]

        z2_codes = tile("z2_codes", [P, N], U32)
        z2_scales = tile("z2_scales", [P, N], U8)
        quantize(z2_codes[:], z2_scales[:], z2)
        xt_g = [gather("xt_g0", xt_w, list3[:, 0:8], U32)]
        xt_s = [gather("xt_s0", xt_srows, list3[:, 0:8], U8)]
        xo_g = gather("xo_g", xo_w, list4[:], U32)
        xo_s = gather("xo_s", xo_srows, list4[:], U8)
        z1_codes = tile("z1_codes", [P, N], U32, "xo_w")
        z1_scales = tile("z1_scales", [P, N], U8)
        for h in range(2):
            quantize(z1_codes[:, h * P : (h + 1) * P], z1_scales[:, h * P : (h + 1) * P], z1[h])
        xt_g.append(gather("xt_g1", xt_w, list3[:, 8:16], U32, "xo_srows"))
        xt_s.append(gather("xt_s1", xt_srows, list3[:, 8:16], U8, "z1_0_woven"))

        def codes_pass(acc, h, ucols, start):
            nc.tensor.matmul_mx(out=acc[:], lhsT=z1_codes[:, h * P : (h + 1) * P].bitcast(E4M3X4), lhsT_scale=z1_scales[:, h * P : (h + 1) * P],
                                rhs=z2_codes[:, ucols].bitcast(E4M3X4), rhs_scale=z2_scales[:, ucols], start=start, stop=not start)

        def vectors_pass(acc, h, ucols, start):
            nc.tensor.matmul_mx(out=acc[:], lhsT=xt_g[h][:].bitcast(E5M2X4), lhsT_scale=xt_s[h][:],
                                rhs=xo_g[:, ucols].bitcast(E4M3X4), rhs_scale=xo_s[:, ucols], start=start, stop=not start)

        acc0 = psum.tile([P, U], F32, name="acc0")
        acc1 = psum.tile([P, P], F32, name="acc1")
        acc2 = psum.tile([P, P], F32, name="acc2")
        vectors_pass(acc0, 0, slice(0, U), True)
        codes_pass(acc0, 0, slice(0, U), False)
        codes_pass(acc1, 1, slice(0, P), True)
        codes_pass(acc2, 1, slice(P, U), True)
        vectors_pass(acc1, 1, slice(0, P), False)
        vectors_pass(acc2, 1, slice(P, U), False)
        res0 = tile("res0", [P, U], F32)
        res1 = tile("res1", [P, P], F32)
        res2 = tile("res2", [P, P], F32)
        nc.scalar.copy(res0[:], acc0[:])
        nc.sync.dma_start(out[0:P, :], res0[:])
        nc.scalar.copy(res1[:], acc1[:])
        nc.scalar.dma_start(out[P:O, 0:P], res1[:])
        nc.vector.tensor_copy(res2[:], acc2[:])
        nc.sync.dma_start(out[P:O, P:U], res2[:])
